import numpy as np, ml_dtypes
CORES = [36,38,116,118,124,126,164,166,244,246,252,254]
N = 12
NH, QP = 12, 32
def setup_inputs(rng):
    return {"q": rng.standard_normal((N, 128, NH * QP), dtype=np.float32).astype(ml_dtypes.bfloat16), "k": rng.standard_normal((N, 128, NH * 128), dtype=np.float32).astype(ml_dtypes.bfloat16), "v": rng.standard_normal((N, 128, NH * 128), dtype=np.float32).astype(ml_dtypes.bfloat16)}
def setup_inputs_big(rng):
    d = setup_inputs(rng)
    for k in ("q", "k", "v"): d[k] = (d[k].astype(np.float32) * 1024.0).astype(d[k].dtype)
    return d
def setup_inputs_small(rng):
    d = setup_inputs(rng)
    for k in ("q", "k", "v"): d[k] = (d[k].astype(np.float32) * (1 / 1024.0)).astype(d[k].dtype)
    return d
def setup_inputs_apart(rng):
    d = setup_inputs(rng)
    f = (10.0 ** rng.permutation(np.linspace(-1.5, 1.5, N))).astype(np.float32).reshape(N, 1, 1)
    for k in ("q", "k", "v"): d[k] = (d[k].astype(np.float32) * f).astype(d[k].dtype)
    return d
def reference(q, k, v):
    Q, K, V = q.astype(np.float64), k.astype(np.float64), v.astype(np.float64)
    y = np.zeros((N, 128, NH * QP))
    for r in range(N):
        for h in range(NH):
            for j in range(N):
                S = np.maximum(K[j][:, 128 * h:128 * h + 128].T @ Q[r][:, QP * h:QP * h + QP], 0.0)
                y[r][:, QP * h:QP * h + QP] += V[j][:, 128 * h:128 * h + 128].T @ S
    return {"y": y.astype(ml_dtypes.bfloat16 if q.dtype != np.float64 else np.float64)}

@@ -1,0 +1,270 @@
+from concourse.bass import DstId, RemoteDMATransfer
+from concourse.mybir import AluOpType
+
+NH, QP, KP = 12, 32, 128
+NCHIP, NPAIR, NUNIT = 6, 3, 3
+
+_BANK = ("psum", [128, 8, 2, QP], "float32")
+SCRATCH = {
+    "ql": ("sbuf", [128, NCHIP, NH, QP], "bfloat16"),
+    "kk": ("sbuf", [128, 2, NH * KP], "bfloat16"),
+    "vv": ("sbuf", [128, 2, NH * KP], "bfloat16"),
+    "zz": ("sbuf", [128, 8, 2, QP], "float32"),
+    "ss": ("sbuf", [128, NPAIR * NUNIT, 8, 2, QP], "bfloat16"),
+    "po": ("sbuf", [128, NCHIP, NH, QP], "bfloat16"),
+    "pl": ("sbuf", [128, NCHIP, NH, QP], "bfloat16"),
+    "yb": ("sbuf", [128, NH, QP], "bfloat16"),
+    "sp0": _BANK, "sp1": _BANK, "sp2": _BANK,
+    "oa0": _BANK, "ob0": _BANK, "oa1": _BANK, "ob1": _BANK,
+    "ac": ("psum", [128, 16, QP], "float32"),
+}
+SEMAPHORES = (["lq", "lk", "lv", "sent", "ka", "kb", "va", "vb", "sZ", "sA", "st"]
+              + ["qa%d" % i for i in range(NCHIP)] + ["pa%d" % i for i in range(NCHIP)]
+              + ["sS%d" % i for i in range(NPAIR * NUNIT)] + ["sR%d" % i for i in range(NPAIR * NUNIT)]
+              + ["sOa%d" % i for i in range(NPAIR)] + ["sOb%d" % i for i in range(NPAIR)]
+              + ["sC%d" % i for i in range(NPAIR)])
+
+_CACHE = {}
+
+
+def _bits(m):
+    return [1 << i for i in range(m.bit_length()) if (m >> i) & 1]
+
+
+def _join(bs):
+    r = 0
+    for b in bs:
+        r |= b
+    return r
+
+
+def _count(m):
+    return len(_bits(m))
+
+
+def _split(masks):
+    used, out = 0, [0] * len(masks)
+    order = sorted(range(len(masks)), key=lambda i: _count(masks[i]))
+    for pos, i in enumerate(order):
+        free = [b for b in _bits(masks[i]) if not b & used]
+        rivals = sum(1 for k in order[pos:] if masks[k] == masks[i])
+        n = 1
+        while n * 2 <= len(free) // rivals:
+            n *= 2
+        out[i] = _join(free[::rivals][:n])
+        used |= out[i]
+    return out
+
+
+def _plan(T, topo):
+    if "plan" in _CACHE:
+        return _CACHE["plan"]
+    cores = list(T.cores)
+    world = range((max(topo.host(c) for c in cores) + 1) * topo.CORES_PER_HOST)
+    sites = []
+    for c in cores:
+        if (topo.host(c), topo.chip(c)) not in sites:
+            sites.append((topo.host(c), topo.chip(c)))
+
+    def free(w):
+        return all(topo.may_write(w, d) for d in cores if d != w)
+
+    plan = []
+    for key in sites:
+        here = [w for w in world if (topo.host(w), topo.chip(w)) == key]
+        ranks = [c for c in cores if c in here]
+        b = [c for c in ranks if free(c)][-1]
+        a = [c for c in ranks if c != b][0]
+        d = [w for w in here if w not in cores and free(w) and topo.die(w) != topo.die(b)][0]
+        plan.append((a, b, d))
+    _CACHE["plan"] = plan
+    return plan
+
+
+def _returns(topo, plan, i, kind, c):
+    src = plan[i][2 - kind]
+    items = []
+    for t in (2 * c, 2 * c + 1):
+        dst = plan[(i + t) % len(plan)][kind]
+        if dst != src:
+            items.append((dst, t))
+    masks = _split([topo.mask(src, d) for d, _ in items])
+    return [(d, t, m) for (d, t), m in zip(items, masks)]
+
+
+def rank_program(g, core, T, topo):
+    plan = _plan(T, topo)
+    n = len(plan)
+    where = [(i, r) for i, abd in enumerate(plan) for r in range(3) if abd[r] == core]
+    if not where:
+        return
+    i, role = where[0]
+    A, B, D = plan[i]
+    S = T.sem
+    te, ve = g.tensor, g.vector
+    sent = [0]
+
+    def one(dst, out, src, sem, mask):
+        rid, pid = topo.addr(dst, core)
+        sent[0] += _count(mask)
+        return RemoteDMATransfer(dst_ids=[DstId(rid=rid, pnc=pid)], dma_engine_mask=mask, remote_sem=sem,
+                                 src=src, dst=out)
+
+    def spread_q():
+        peers = [((i - t) % n, t) for t in range(1, n)]
+        col = role
+        mask = topo.mask(core, plan[peers[0][0]][col])
+        for x, _ in peers:
+            mask &= topo.mask(core, plan[x][col])
+        ids = []
+        for x, _ in peers:
+            rid, pid = topo.addr(plan[x][col], core)
+            ids.append(DstId(rid=rid, pnc=pid))
+        sent[0] += _count(mask)
+        g.remote_dma_fused([RemoteDMATransfer(dst_ids=ids, dma_engine_mask=mask, remote_sem=S["qa%d" % i],
+                                              srcs=[T.ql[:, 0]], dsts=[T.ql[:, t] for _, t in peers])],
+                           local_sem=S.sent)
+
+    hand = _join(_bits(topo.mask(A, D))[::2])
+    kv_a = _split([topo.mask(A, D), topo.mask(A, B)])
+    kv_b = topo.mask(B, D)
+
+    if role < 2:
+        g.sync.dma_start(T.ql[:, 0], T.q[:]).then_inc(S.lq, 16)
+        g.scalar.dma_start(T.kk[:, role], T.k[:]).then_inc(S.lk, 16)
+        g.sync.dma_start(T.vv[:, role], T.v[:]).then_inc(S.lv, 16)
+
+    if role == 0:
+        g.wait_ge(S.lq, 16)
+        g.remote_dma_fused([one(D, T.ql[:, 0], T.ql[:, 0], S["qa%d" % i], hand)], local_sem=S.sent)
+        g.wait_ge(S.lk, 16)
+        g.remote_dma_fused([one(D, T.kk[:, 0], T.kk[:, 0], S.ka, kv_a[0]),
+                            one(B, T.kk[:, 0], T.kk[:, 0], S.ka, kv_a[1])], local_sem=S.sent)
+        g.wait_ge(S.lv, 16)
+        g.remote_dma_fused([one(D, T.vv[:, 0], T.vv[:, 0], S.va, kv_a[0]),
+                            one(B, T.vv[:, 0], T.vv[:, 0], S.va, kv_a[1])], local_sem=S.sent)
+    elif role == 1:
+        g.wait_ge(S.lq, 16)
+        spread_q()
+        g.wait_ge(S.lk, 16)
+        g.remote_dma_fused([one(D, T.kk[:, 1], T.kk[:, 1], S.kb, kv_b)], local_sem=S.sent)
+        g.wait_ge(S.lv, 16)
+        g.remote_dma_fused([one(D, T.vv[:, 1], T.vv[:, 1], S.vb, kv_b)], local_sem=S.sent)
+    else:
+        g.wait_ge(S["qa%d" % i], _count(hand))
+        spread_q()
+
+    if role > 0:
+        kind = 2 - role
+        col = role
+        sp = [T.sp0, T.sp1, T.sp2]
+        oa, ob = [T.oa0, T.oa1], [T.ob0, T.ob1]
+        far = topo.mask(core, plan[(i + 1) % n][col])
+        for x in range(n):
+            if x != i:
+                far &= topo.mask(plan[x][col], core)
+        q_wait = [(S.lq, 16) if role == 1 else (S["qa%d" % i], _count(hand))]
+        q_wait += [(S["qa%d" % ((i + t) % n)], _count(far)) for t in range(1, n)]
+        if role == 1:
+            k_wait = [(S.lk, 16), (S.ka, _count(kv_a[1]))]
+            v_wait = [(S.lv, 16), (S.va, _count(kv_a[1]))]
+        else:
+            k_wait = [(S.ka, _count(kv_a[0])), (S.kb, _count(kv_b))]
+            v_wait = [(S.va, _count(kv_a[0])), (S.vb, _count(kv_b))]
+
+        def s_unit(c, u):
+            gu = NUNIT * c + u
+            if u == 0:
+                te.wait_ge(*q_wait[2 * c])
+                te.wait_ge(*q_wait[2 * c + 1])
+                if c == 0:
+                    for w in k_wait:
+                        te.wait_ge(*w)
+            if c > 0:
+                te.wait_ge(S["sR%d" % (gu - NUNIT)], 1)
+            for hl in range(4):
+                h = 4 * u + hl
+                for j in range(2):
+                    te.matmul(sp[u][:, 2 * hl + j], T.kk[:, j, KP * h:KP * h + KP], T.ql[:, 2 * c:2 * c + 2, h, :],
+                              start=True, stop=True).then_inc(S["sS%d" % gu], 1)
+
+        def o_unit(c, u):
+            gu = NUNIT * c + u
+            te.wait_ge(S["sR%d" % gu], 1)
+            if c == 0 and u == 0:
+                for w in v_wait:
+                    te.wait_ge(*w)
+            if c >= 2 and u == 0:
+                te.wait_ge(S["sC%d" % (c - 2)], 4)
+            for hl in range(4):
+                h = 4 * u + hl
+                bank = oa[c % 2] if h < 8 else ob[c % 2]
+                for j in range(2):
+                    te.matmul(bank[:, h % 8], T.vv[:, j, KP * h:KP * h + KP], T.ss[:, gu, 2 * hl + j],
+                              start=(j == 0), stop=(j == 1)).then_inc(S[("sOa%d" if h < 8 else "sOb%d") % c], 1)
+
+        def relu(c, u):
+            gu = NUNIT * c + u
+            ve.wait_ge(S["sS%d" % gu], 8)
+            ve.tensor_tensor(T.ss[:, gu], sp[u][:], T.zz[:], AluOpType.max).then_inc(S["sR%d" % gu], 1)
+
+        def block(t):
+            return T.pl if plan[(i + t) % n][kind] == core else T.po
+
+        def copy_a(c):
+            ve.wait_ge(S["sOa%d" % c], 16)
+            for r in range(2):
+                t = 2 * c + r
+                ve.tensor_copy(block(t)[:, t, 0:8, :], oa[c % 2][:, :, r, :]).then_inc(S["sC%d" % c], 1)
+
+        def copy_b(c):
+            ve.wait_ge(S["sOb%d" % c], 8)
+            for r in range(2):
+                t = 2 * c + r
+                ve.tensor_copy(block(t)[:, t, 8:12, :], ob[c % 2][:, 0:4, r, :]).then_inc(S["sC%d" % c], 1)
+
+        for u in range(NUNIT):
+            s_unit(0, u)
+        for c in range(NPAIR):
+            for u in range(NUNIT):
+                o_unit(c, u)
+                if c + 1 < NPAIR:
+                    s_unit(c + 1, u)
+        ve.memset(T.zz[:], 0.0).then_inc(S.sZ, 1)
+        ve.wait_ge(S.sZ, 1)
+        for u in range(NUNIT):
+            relu(0, u)
+        for c in range(NPAIR):
+            if c + 1 < NPAIR:
+                relu(c + 1, 0)
+            copy_a(c)
+            if c + 1 < NPAIR:
+                relu(c + 1, 1)
+            copy_b(c)
+            if c + 1 < NPAIR:
+                relu(c + 1, 2)
+        for c in range(NPAIR):
+            g.wait_ge(S["sC%d" % c], 4)
+            g.remote_dma_fused([one(d, T.pl[:, t], T.po[:, t], S["pa%d" % t], m)
+                                for d, t, m in _returns(topo, plan, i, kind, c)], local_sem=S.sent)
+
+    if role < 2:
+        for t in range(n):
+            src = (i - t) % n
+            got = [m for d, tt, m in _returns(topo, plan, src, role, t // 2) if tt == t and d == core]
+            if got:
+                ve.wait_ge(S["pa%d" % t], _count(got[0]))
+            else:
+                ve.wait_ge(S["sC%d" % (t // 2)], 4)
+            if t == 0:
+                continue
+            if t > 1:
+                ve.wait_ge(S.sA, t - 1)
+            out = T.yb[:] if t == n - 1 else T.ac[:, 0:NH, :]
+            in0 = T.pl[:, 0] if t == 1 else T.ac[:, 0:NH, :]
+            ve.tensor_tensor(out, in0, T.pl[:, t], AluOpType.add).then_inc(S.sA, 1)
+        g.sync.wait_ge(S.sA, n - 1)
+        g.sync.dma_start(T.y[:], T.yb[:]).then_inc(S.st, 16)
+        g.sync.wait_ge(S.st, 16)
+
+    g.wait_ge(S.sent, sent[0])

@@ -2,29 +2,33 @@ from concourse.bass import DstId, RemoteDMATransfer
 from concourse.mybir import AluOpType
 
 NH, QP, KP = 12, 32, 128
-NCHIP, NPAIR, NUNIT = 6, 3, 3
+HH = NH // 2
+NCHIP, NPAIR, NUNIT = 6, 3, 2
+UH = HH // NUNIT
+NSB = 4
 
 _BANK = ("psum", [128, 8, 2, QP], "float32")
 SCRATCH = {
     "ql": ("sbuf", [128, NCHIP, NH, QP], "bfloat16"),
     "kk": ("sbuf", [128, 2, NH * KP], "bfloat16"),
     "vv": ("sbuf", [128, 2, NH * KP], "bfloat16"),
-    "zz": ("sbuf", [128, 8, 2, QP], "float32"),
-    "ss": ("sbuf", [128, NPAIR * NUNIT, 8, 2, QP], "bfloat16"),
+    "zz": ("sbuf", [128, 2 * UH, 2, QP], "float32"),
+    "ss": ("sbuf", [128, NPAIR * NUNIT, 2 * UH, 2, QP], "bfloat16"),
     "po": ("sbuf", [128, NCHIP, NH, QP], "bfloat16"),
     "pl": ("sbuf", [128, NCHIP, NH, QP], "bfloat16"),
     "yb": ("sbuf", [128, NH, QP], "bfloat16"),
-    "sp0": _BANK, "sp1": _BANK, "sp2": _BANK,
-    "oa0": _BANK, "ob0": _BANK, "oa1": _BANK, "ob1": _BANK,
+    "sp0": _BANK, "sp1": _BANK, "sp2": _BANK, "sp3": _BANK,
+    "oc0": _BANK, "oc1": _BANK, "oc2": _BANK,
     "ac": ("psum", [128, 16, QP], "float32"),
 }
 SEMAPHORES = (["lq", "lk", "lv", "sent", "ka", "kb", "va", "vb", "sZ", "sA", "st"]
               + ["qa%d" % i for i in range(NCHIP)] + ["pa%d" % i for i in range(NCHIP)]
               + ["sS%d" % i for i in range(NPAIR * NUNIT)] + ["sR%d" % i for i in range(NPAIR * NUNIT)]
-              + ["sOa%d" % i for i in range(NPAIR)] + ["sOb%d" % i for i in range(NPAIR)]
-              + ["sC%d" % i for i in range(NPAIR)])
+              + ["sO%d" % i for i in range(NPAIR)] + ["sC%d" % i for i in range(NPAIR)])
 
 _CACHE = {}
+_WORK = {1: (1, 0), 2: (0, 0), 3: (1, 1), 4: (0, 1)}
+_ROLE = {v: k for k, v in _WORK.items()}
 
 
 def _bits(m):
@@ -75,14 +79,16 @@ def _plan(T, topo):
         ranks = [c for c in cores if c in here]
         b = [c for c in ranks if free(c)][-1]
         a = [c for c in ranks if c != b][0]
-        d = [w for w in here if w not in cores and free(w) and topo.die(w) != topo.die(b)][0]
-        plan.append((a, b, d))
+        aid = [w for w in here if w not in cores and free(w)]
+        near = [w for w in aid if topo.die(w) == topo.die(b)]
+        over = [w for w in aid if topo.die(w) != topo.die(b)]
+        plan.append((a, b, over[0], near[0], over[1]))
     _CACHE["plan"] = plan
     return plan
 
 
-def _returns(topo, plan, i, kind, c):
-    src = plan[i][2 - kind]
+def _returns(topo, plan, i, kind, s, c):
+    src = plan[i][_ROLE[(kind, s)]]
     items = []
     for t in (2 * c, 2 * c + 1):
         dst = plan[(i + t) % len(plan)][kind]
@@ -95,14 +101,21 @@ def _returns(topo, plan, i, kind, c):
 def rank_program(g, core, T, topo):
     plan = _plan(T, topo)
     n = len(plan)
-    where = [(i, r) for i, abd in enumerate(plan) for r in range(3) if abd[r] == core]
+    where = [(i, r) for i, row in enumerate(plan) for r in range(len(row)) if row[r] == core]
     if not where:
         return
     i, role = where[0]
-    A, B, D = plan[i]
+    A, B, D, B2, D2 = plan[i]
     S = T.sem
     te, ve = g.tensor, g.vector
     sent = [0]
+    my_q = S["qa%d" % i]
+
+    def hs(s):
+        return slice(HH * s, HH * s + HH)
+
+    def ks(s):
+        return slice(HH * KP * s, HH * KP * (s + 1))
 
     def one(dst, out, src, sem, mask):
         rid, pid = topo.addr(dst, core)
@@ -110,24 +123,28 @@ def rank_program(g, core, T, topo):
         return RemoteDMATransfer(dst_ids=[DstId(rid=rid, pnc=pid)], dma_engine_mask=mask, remote_sem=sem,
                                  src=src, dst=out)
 
-    def spread_q():
+    def far_mask(src_role, x):
+        m = topo.mask(plan[x][src_role], plan[(x + 1) % n][src_role])
+        for y in range(n):
+            if y != x:
+                m &= topo.mask(plan[x][src_role], plan[y][src_role])
+        return m
+
+    def spread_q(s, mask):
         peers = [((i - t) % n, t) for t in range(1, n)]
-        col = role
-        mask = topo.mask(core, plan[peers[0][0]][col])
-        for x, _ in peers:
-            mask &= topo.mask(core, plan[x][col])
         ids = []
         for x, _ in peers:
-            rid, pid = topo.addr(plan[x][col], core)
+            rid, pid = topo.addr(plan[x][role], core)
             ids.append(DstId(rid=rid, pnc=pid))
         sent[0] += _count(mask)
-        g.remote_dma_fused([RemoteDMATransfer(dst_ids=ids, dma_engine_mask=mask, remote_sem=S["qa%d" % i],
-                                              srcs=[T.ql[:, 0]], dsts=[T.ql[:, t] for _, t in peers])],
-                           local_sem=S.sent)
+        return RemoteDMATransfer(dst_ids=ids, dma_engine_mask=mask, remote_sem=my_q,
+                                 srcs=[T.ql[:, 0, hs(s), :]], dsts=[T.ql[:, t, hs(s), :] for _, t in peers])
 
-    hand = _join(_bits(topo.mask(A, D))[::2])
-    kv_a = _split([topo.mask(A, D), topo.mask(A, B)])
-    kv_b = topo.mask(B, D)
+    hb = _bits(topo.mask(A, D) & topo.mask(A, D2))[::2]
+    hand_a = [_join(hb[0::2]), _join(hb[1::2])]
+    q_b = _split([far_mask(1, i), topo.mask(B, B2)])
+    kv_a = _split([topo.mask(A, D), topo.mask(A, B), topo.mask(A, D2), topo.mask(A, B2)])
+    kv_b = _split([topo.mask(B, B2), topo.mask(B, D), topo.mask(B, D2)])
 
     if role < 2:
         g.sync.dma_start(T.ql[:, 0], T.q[:]).then_inc(S.lq, 16)
@@ -136,41 +153,41 @@ def rank_program(g, core, T, topo):
 
     if role == 0:
         g.wait_ge(S.lq, 16)
-        g.remote_dma_fused([one(D, T.ql[:, 0], T.ql[:, 0], S["qa%d" % i], hand)], local_sem=S.sent)
-        g.wait_ge(S.lk, 16)
-        g.remote_dma_fused([one(D, T.kk[:, 0], T.kk[:, 0], S.ka, kv_a[0]),
-                            one(B, T.kk[:, 0], T.kk[:, 0], S.ka, kv_a[1])], local_sem=S.sent)
-        g.wait_ge(S.lv, 16)
-        g.remote_dma_fused([one(D, T.vv[:, 0], T.vv[:, 0], S.va, kv_a[0]),
-                            one(B, T.vv[:, 0], T.vv[:, 0], S.va, kv_a[1])], local_sem=S.sent)
+        g.remote_dma_fused([one(D, T.ql[:, 0, hs(0), :], T.ql[:, 0, hs(0), :], my_q, hand_a[0]),
+                            one(D2, T.ql[:, 0, hs(1), :], T.ql[:, 0, hs(1), :], my_q, hand_a[1])], local_sem=S.sent)
+        for buf, ld, sem in ((T.kk, S.lk, S.ka), (T.vv, S.lv, S.va)):
+            g.wait_ge(ld, 16)
+            g.remote_dma_fused([one(D, buf[:, 0, ks(0)], buf[:, 0, ks(0)], sem, kv_a[0]),
+                                one(B, buf[:, 0, ks(0)], buf[:, 0, ks(0)], sem, kv_a[1]),
+                                one(D2, buf[:, 0, ks(1)], buf[:, 0, ks(1)], sem, kv_a[2]),
+                                one(B2, buf[:, 0, ks(1)], buf[:, 0, ks(1)], sem, kv_a[3])], local_sem=S.sent)
     elif role == 1:
         g.wait_ge(S.lq, 16)
-        spread_q()
-        g.wait_ge(S.lk, 16)
-        g.remote_dma_fused([one(D, T.kk[:, 1], T.kk[:, 1], S.kb, kv_b)], local_sem=S.sent)
-        g.wait_ge(S.lv, 16)
-        g.remote_dma_fused([one(D, T.vv[:, 1], T.vv[:, 1], S.vb, kv_b)], local_sem=S.sent)
-    else:
-        g.wait_ge(S["qa%d" % i], _count(hand))
-        spread_q()
+        g.remote_dma_fused([spread_q(0, q_b[0]),
+                            one(B2, T.ql[:, 0, hs(1), :], T.ql[:, 0, hs(1), :], my_q, q_b[1])], local_sem=S.sent)
+        for buf, ld, sem in ((T.kk, S.lk, S.kb), (T.vv, S.lv, S.vb)):
+            g.wait_ge(ld, 16)
+            g.remote_dma_fused([one(B2, buf[:, 1, ks(1)], buf[:, 1, ks(1)], sem, kv_b[0]),
+                                one(D, buf[:, 1, ks(0)], buf[:, 1, ks(0)], sem, kv_b[1]),
+                                one(D2, buf[:, 1, ks(1)], buf[:, 1, ks(1)], sem, kv_b[2])], local_sem=S.sent)
 
     if role > 0:
-        kind = 2 - role
-        col = role
-        sp = [T.sp0, T.sp1, T.sp2]
-        oa, ob = [T.oa0, T.oa1], [T.ob0, T.ob1]
-        far = topo.mask(core, plan[(i + 1) % n][col])
-        for x in range(n):
-            if x != i:
-                far &= topo.mask(plan[x][col], core)
-        q_wait = [(S.lq, 16) if role == 1 else (S["qa%d" % i], _count(hand))]
-        q_wait += [(S["qa%d" % ((i + t) % n)], _count(far)) for t in range(1, n)]
-        if role == 1:
-            k_wait = [(S.lk, 16), (S.ka, _count(kv_a[1]))]
-            v_wait = [(S.lv, 16), (S.va, _count(kv_a[1]))]
-        else:
-            k_wait = [(S.ka, _count(kv_a[0])), (S.kb, _count(kv_b))]
-            v_wait = [(S.va, _count(kv_a[0])), (S.vb, _count(kv_b))]
+        kind, s = _WORK[role]
+        own_q = {1: (S.lq, 16), 2: (my_q, _count(hand_a[0])), 3: (my_q, _count(q_b[1])), 4: (my_q, _count(hand_a[1]))}[role]
+        if role != 1:
+            g.wait_ge(*own_q)
+            g.remote_dma_fused([spread_q(s, far_mask(role, i))], local_sem=S.sent)
+        sp = [T.sp0, T.sp1, T.sp2, T.sp3]
+        oc = [T.oc0, T.oc1, T.oc2]
+        q_wait = [own_q]
+        for t in range(1, n):
+            x = (i + t) % n
+            m = _split([far_mask(1, x), topo.mask(plan[x][1], plan[x][3])])[0] if role == 1 else far_mask(role, x)
+            q_wait.append((S["qa%d" % x], _count(m)))
+        from_a = {1: kv_a[1], 2: kv_a[0], 3: kv_a[3], 4: kv_a[2]}[role]
+        from_b = {1: None, 2: kv_b[1], 3: kv_b[0], 4: kv_b[2]}[role]
+        k_wait = [(S.ka, _count(from_a)), (S.lk, 16) if role == 1 else (S.kb, _count(from_b))]
+        v_wait = [(S.va, _count(from_a)), (S.lv, 16) if role == 1 else (S.vb, _count(from_b))]
 
         def s_unit(c, u):
             gu = NUNIT * c + u
@@ -180,13 +197,13 @@ def rank_program(g, core, T, topo):
                 if c == 0:
                     for w in k_wait:
                         te.wait_ge(*w)
-            if c > 0:
-                te.wait_ge(S["sR%d" % (gu - NUNIT)], 1)
-            for hl in range(4):
-                h = 4 * u + hl
+            if gu >= NSB:
+                te.wait_ge(S["sR%d" % (gu - NSB)], 1)
+            for hl in range(UH):
+                h = HH * s + UH * u + hl
                 for j in range(2):
-                    te.matmul(sp[u][:, 2 * hl + j], T.kk[:, j, KP * h:KP * h + KP], T.ql[:, 2 * c:2 * c + 2, h, :],
-                              start=True, stop=True).then_inc(S["sS%d" % gu], 1)
+                    te.matmul(sp[gu % NSB][:, 2 * hl + j], T.kk[:, j, KP * h:KP * h + KP],
+                              T.ql[:, 2 * c:2 * c + 2, h, :], start=True, stop=True).then_inc(S["sS%d" % gu], 1)
 
         def o_unit(c, u):
             gu = NUNIT * c + u
@@ -194,34 +211,23 @@ def rank_program(g, core, T, topo):
             if c == 0 and u == 0:
                 for w in v_wait:
                     te.wait_ge(*w)
-            if c >= 2 and u == 0:
-                te.wait_ge(S["sC%d" % (c - 2)], 4)
-            for hl in range(4):
-                h = 4 * u + hl
-                bank = oa[c % 2] if h < 8 else ob[c % 2]
+            for hl in range(UH):
+                h = HH * s + UH * u + hl
                 for j in range(2):
-                    te.matmul(bank[:, h % 8], T.vv[:, j, KP * h:KP * h + KP], T.ss[:, gu, 2 * hl + j],
-                              start=(j == 0), stop=(j == 1)).then_inc(S[("sOa%d" if h < 8 else "sOb%d") % c], 1)
+                    te.matmul(oc[c][:, UH * u + hl], T.vv[:, j, KP * h:KP * h + KP], T.ss[:, gu, 2 * hl + j],
+                              start=(j == 0), stop=(j == 1)).then_inc(S["sO%d" % c], 1)
 
         def relu(c, u):
             gu = NUNIT * c + u
-            ve.wait_ge(S["sS%d" % gu], 8)
-            ve.tensor_tensor(T.ss[:, gu], sp[u][:], T.zz[:], AluOpType.max).then_inc(S["sR%d" % gu], 1)
+            ve.wait_ge(S["sS%d" % gu], 2 * UH)
+            ve.tensor_tensor(T.ss[:, gu], sp[gu % NSB][:, 0:2 * UH], T.zz[:], AluOpType.max).then_inc(S["sR%d" % gu], 1)
 
-        def block(t):
-            return T.pl if plan[(i + t) % n][kind] == core else T.po
-
-        def copy_a(c):
-            ve.wait_ge(S["sOa%d" % c], 16)
+        def copy(c):
+            ve.wait_ge(S["sO%d" % c], 2 * HH)
             for r in range(2):
                 t = 2 * c + r
-                ve.tensor_copy(block(t)[:, t, 0:8, :], oa[c % 2][:, :, r, :]).then_inc(S["sC%d" % c], 1)
-
-        def copy_b(c):
-            ve.wait_ge(S["sOb%d" % c], 8)
-            for r in range(2):
-                t = 2 * c + r
-                ve.tensor_copy(block(t)[:, t, 8:12, :], ob[c % 2][:, 0:4, r, :]).then_inc(S["sC%d" % c], 1)
+                buf = T.pl if plan[(i + t) % n][kind] == core else T.po
+                ve.tensor_copy(buf[:, t, hs(s), :], oc[c][:, 0:HH, r, :]).then_inc(S["sC%d" % c], 1)
 
         for u in range(NUNIT):
             s_unit(0, u)
@@ -237,25 +243,25 @@ def rank_program(g, core, T, topo):
         for c in range(NPAIR):
             if c + 1 < NPAIR:
                 relu(c + 1, 0)
-            copy_a(c)
+            copy(c)
             if c + 1 < NPAIR:
                 relu(c + 1, 1)
-            copy_b(c)
-            if c + 1 < NPAIR:
-                relu(c + 1, 2)
         for c in range(NPAIR):
-            g.wait_ge(S["sC%d" % c], 4)
-            g.remote_dma_fused([one(d, T.pl[:, t], T.po[:, t], S["pa%d" % t], m)
-                                for d, t, m in _returns(topo, plan, i, kind, c)], local_sem=S.sent)
+            g.wait_ge(S["sC%d" % c], 2)
+            g.remote_dma_fused([one(d, T.pl[:, t, hs(s), :], T.po[:, t, hs(s), :], S["pa%d" % t], m)
+                                for d, t, m in _returns(topo, plan, i, kind, s, c)], local_sem=S.sent)
 
     if role < 2:
         for t in range(n):
             src = (i - t) % n
-            got = [m for d, tt, m in _returns(topo, plan, src, role, t // 2) if tt == t and d == core]
-            if got:
-                ve.wait_ge(S["pa%d" % t], _count(got[0]))
-            else:
-                ve.wait_ge(S["sC%d" % (t // 2)], 4)
+            got = 0
+            for s in range(2):
+                hit = [m for d, tt, m in _returns(topo, plan, src, role, s, t // 2) if tt == t and d == core]
+                if hit:
+                    got += _count(hit[0])
+                else:
+                    ve.wait_ge(S["sC%d" % (t // 2)], 2)
+            ve.wait_ge(S["pa%d" % t], got)
             if t == 0:
                 continue
             if t > 1:

from concourse.bass import DstId, RemoteDMATransfer
from concourse.mybir import AluOpType

NH, QP, KP = 12, 32, 128
HH = NH // 2
NCHIP, NPAIR, NUNIT = 6, 3, 2
UH = HH // NUNIT
NSB = 4

_BANK = ("psum", [128, 8, 2, QP], "float32")
SCRATCH = {
    "ql": ("sbuf", [128, NCHIP, NH, QP], "bfloat16"),
    "kk": ("sbuf", [128, 2, NH * KP], "bfloat16"),
    "vv": ("sbuf", [128, 2, NH * KP], "bfloat16"),
    "zz": ("sbuf", [128, 2 * UH, 2, QP], "float32"),
    "ss": ("sbuf", [128, NPAIR * NUNIT, 2 * UH, 2, QP], "bfloat16"),
    "po": ("sbuf", [128, NCHIP, NH, QP], "bfloat16"),
    "pl": ("sbuf", [128, NCHIP, NH, QP], "bfloat16"),
    "yb": ("sbuf", [128, NH, QP], "bfloat16"),
    "sp0": _BANK, "sp1": _BANK, "sp2": _BANK, "sp3": _BANK,
    "oc0": _BANK, "oc1": _BANK, "oc2": _BANK,
    "ac": ("psum", [128, 16, QP], "float32"),
}
SEMAPHORES = (["lq", "lk", "lv", "sent", "ka", "kb", "va", "vb", "sZ", "sA", "st"]
              + ["qa%d" % i for i in range(NCHIP)] + ["pa%d" % i for i in range(NCHIP)]
              + ["sS%d" % i for i in range(NPAIR * NUNIT)] + ["sR%d" % i for i in range(NPAIR * NUNIT)]
              + ["sO%d" % i for i in range(NPAIR)] + ["sC%d" % i for i in range(NPAIR)])

_CACHE = {}
_WORK = {1: (1, 0), 2: (0, 0), 3: (1, 1), 4: (0, 1)}
_ROLE = {v: k for k, v in _WORK.items()}


def _bits(m):
    return [1 << i for i in range(m.bit_length()) if (m >> i) & 1]


def _join(bs):
    r = 0
    for b in bs:
        r |= b
    return r


def _count(m):
    return len(_bits(m))


def _split(masks):
    used, out = 0, [0] * len(masks)
    order = sorted(range(len(masks)), key=lambda i: _count(masks[i]))
    for pos, i in enumerate(order):
        free = [b for b in _bits(masks[i]) if not b & used]
        rivals = sum(1 for k in order[pos:] if masks[k] == masks[i])
        n = 1
        while n * 2 <= len(free) // rivals:
            n *= 2
        out[i] = _join(free[::rivals][:n])
        used |= out[i]
    return out


def _plan(T, topo):
    if "plan" in _CACHE:
        return _CACHE["plan"]
    cores = list(T.cores)
    world = range((max(topo.host(c) for c in cores) + 1) * topo.CORES_PER_HOST)
    sites = []
    for c in cores:
        if (topo.host(c), topo.chip(c)) not in sites:
            sites.append((topo.host(c), topo.chip(c)))

    def free(w):
        return all(topo.may_write(w, d) for d in cores if d != w)

    plan = []
    for key in sites:
        here = [w for w in world if (topo.host(w), topo.chip(w)) == key]
        ranks = [c for c in cores if c in here]
        b = [c for c in ranks if free(c)][-1]
        a = [c for c in ranks if c != b][0]
        aid = [w for w in here if w not in cores and free(w)]
        near = [w for w in aid if topo.die(w) == topo.die(b)]
        over = [w for w in aid if topo.die(w) != topo.die(b)]
        plan.append((a, b, over[0], near[0], over[1]))
    _CACHE["plan"] = plan
    return plan


def _returns(topo, plan, i, kind, s, c):
    src = plan[i][_ROLE[(kind, s)]]
    items = []
    for t in (2 * c, 2 * c + 1):
        dst = plan[(i + t) % len(plan)][kind]
        if dst != src:
            items.append((dst, t))
    masks = _split([topo.mask(src, d) for d, _ in items])
    return [(d, t, m) for (d, t), m in zip(items, masks)]


def rank_program(g, core, T, topo):
    plan = _plan(T, topo)
    n = len(plan)
    where = [(i, r) for i, row in enumerate(plan) for r in range(len(row)) if row[r] == core]
    if not where:
        return
    i, role = where[0]
    A, B, D, B2, D2 = plan[i]
    S = T.sem
    te, ve = g.tensor, g.vector
    sent = [0]
    my_q = S["qa%d" % i]

    def hs(s):
        return slice(HH * s, HH * s + HH)

    def ks(s):
        return slice(HH * KP * s, HH * KP * (s + 1))

    def one(dst, out, src, sem, mask):
        rid, pid = topo.addr(dst, core)
        sent[0] += _count(mask)
        return RemoteDMATransfer(dst_ids=[DstId(rid=rid, pnc=pid)], dma_engine_mask=mask, remote_sem=sem,
                                 src=src, dst=out)

    def far_mask(src_role, x):
        m = topo.mask(plan[x][src_role], plan[(x + 1) % n][src_role])
        for y in range(n):
            if y != x:
                m &= topo.mask(plan[x][src_role], plan[y][src_role])
        return m

    def spread_q(s, mask):
        peers = [((i - t) % n, t) for t in range(1, n)]
        ids = []
        for x, _ in peers:
            rid, pid = topo.addr(plan[x][role], core)
            ids.append(DstId(rid=rid, pnc=pid))
        sent[0] += _count(mask)
        return RemoteDMATransfer(dst_ids=ids, dma_engine_mask=mask, remote_sem=my_q,
                                 srcs=[T.ql[:, 0, hs(s), :]], dsts=[T.ql[:, t, hs(s), :] for _, t in peers])

    hb = _bits(topo.mask(A, D) & topo.mask(A, D2))[::2]
    hand_a = [_join(hb[0::2]), _join(hb[1::2])]
    q_b = _split([far_mask(1, i), topo.mask(B, B2)])
    kv_a = _split([topo.mask(A, D), topo.mask(A, B), topo.mask(A, D2), topo.mask(A, B2)])
    kv_b = _split([topo.mask(B, B2), topo.mask(B, D), topo.mask(B, D2)])

    if role < 2:
        g.sync.dma_start(T.ql[:, 0], T.q[:]).then_inc(S.lq, 16)
        g.scalar.dma_start(T.kk[:, role], T.k[:]).then_inc(S.lk, 16)
        g.sync.dma_start(T.vv[:, role], T.v[:]).then_inc(S.lv, 16)

    if role == 0:
        g.wait_ge(S.lq, 16)
        g.remote_dma_fused([one(D, T.ql[:, 0, hs(0), :], T.ql[:, 0, hs(0), :], my_q, hand_a[0]),
                            one(D2, T.ql[:, 0, hs(1), :], T.ql[:, 0, hs(1), :], my_q, hand_a[1])], local_sem=S.sent)
        for buf, ld, sem in ((T.kk, S.lk, S.ka), (T.vv, S.lv, S.va)):
            g.wait_ge(ld, 16)
            g.remote_dma_fused([one(D, buf[:, 0, ks(0)], buf[:, 0, ks(0)], sem, kv_a[0]),
                                one(B, buf[:, 0, ks(0)], buf[:, 0, ks(0)], sem, kv_a[1]),
                                one(D2, buf[:, 0, ks(1)], buf[:, 0, ks(1)], sem, kv_a[2]),
                                one(B2, buf[:, 0, ks(1)], buf[:, 0, ks(1)], sem, kv_a[3])], local_sem=S.sent)
    elif role == 1:
        g.wait_ge(S.lq, 16)
        g.remote_dma_fused([spread_q(0, q_b[0]),
                            one(B2, T.ql[:, 0, hs(1), :], T.ql[:, 0, hs(1), :], my_q, q_b[1])], local_sem=S.sent)
        for buf, ld, sem in ((T.kk, S.lk, S.kb), (T.vv, S.lv, S.vb)):
            g.wait_ge(ld, 16)
            g.remote_dma_fused([one(B2, buf[:, 1, ks(1)], buf[:, 1, ks(1)], sem, kv_b[0]),
                                one(D, buf[:, 1, ks(0)], buf[:, 1, ks(0)], sem, kv_b[1]),
                                one(D2, buf[:, 1, ks(1)], buf[:, 1, ks(1)], sem, kv_b[2])], local_sem=S.sent)

    if role > 0:
        kind, s = _WORK[role]
        own_q = {1: (S.lq, 16), 2: (my_q, _count(hand_a[0])), 3: (my_q, _count(q_b[1])), 4: (my_q, _count(hand_a[1]))}[role]
        if role != 1:
            g.wait_ge(*own_q)
            g.remote_dma_fused([spread_q(s, far_mask(role, i))], local_sem=S.sent)
        sp = [T.sp0, T.sp1, T.sp2, T.sp3]
        oc = [T.oc0, T.oc1, T.oc2]
        q_wait = [own_q]
        for t in range(1, n):
            x = (i + t) % n
            m = _split([far_mask(1, x), topo.mask(plan[x][1], plan[x][3])])[0] if role == 1 else far_mask(role, x)
            q_wait.append((S["qa%d" % x], _count(m)))
        from_a = {1: kv_a[1], 2: kv_a[0], 3: kv_a[3], 4: kv_a[2]}[role]
        from_b = {1: None, 2: kv_b[1], 3: kv_b[0], 4: kv_b[2]}[role]
        k_wait = [(S.ka, _count(from_a)), (S.lk, 16) if role == 1 else (S.kb, _count(from_b))]
        v_wait = [(S.va, _count(from_a)), (S.lv, 16) if role == 1 else (S.vb, _count(from_b))]

        def s_unit(c, u):
            gu = NUNIT * c + u
            if u == 0:
                te.wait_ge(*q_wait[2 * c])
                te.wait_ge(*q_wait[2 * c + 1])
                if c == 0:
                    for w in k_wait:
                        te.wait_ge(*w)
            if gu >= NSB:
                te.wait_ge(S["sR%d" % (gu - NSB)], 1)
            for hl in range(UH):
                h = HH * s + UH * u + hl
                for j in range(2):
                    te.matmul(sp[gu % NSB][:, 2 * hl + j], T.kk[:, j, KP * h:KP * h + KP],
                              T.ql[:, 2 * c:2 * c + 2, h, :], start=True, stop=True).then_inc(S["sS%d" % gu], 1)

        def o_unit(c, u):
            gu = NUNIT * c + u
            te.wait_ge(S["sR%d" % gu], 1)
            if c == 0 and u == 0:
                for w in v_wait:
                    te.wait_ge(*w)
            for hl in range(UH):
                h = HH * s + UH * u + hl
                for j in range(2):
                    te.matmul(oc[c][:, UH * u + hl], T.vv[:, j, KP * h:KP * h + KP], T.ss[:, gu, 2 * hl + j],
                              start=(j == 0), stop=(j == 1)).then_inc(S["sO%d" % c], 1)

        def relu(c, u):
            gu = NUNIT * c + u
            ve.wait_ge(S["sS%d" % gu], 2 * UH)
            ve.tensor_tensor(T.ss[:, gu], sp[gu % NSB][:, 0:2 * UH], T.zz[:], AluOpType.max).then_inc(S["sR%d" % gu], 1)

        def copy(c):
            ve.wait_ge(S["sO%d" % c], 2 * HH)
            for r in range(2):
                t = 2 * c + r
                buf = T.pl if plan[(i + t) % n][kind] == core else T.po
                ve.tensor_copy(buf[:, t, hs(s), :], oc[c][:, 0:HH, r, :]).then_inc(S["sC%d" % c], 1)

        for u in range(NUNIT):
            s_unit(0, u)
        for c in range(NPAIR):
            for u in range(NUNIT):
                o_unit(c, u)
                if c + 1 < NPAIR:
                    s_unit(c + 1, u)
        ve.memset(T.zz[:], 0.0).then_inc(S.sZ, 1)
        ve.wait_ge(S.sZ, 1)
        for u in range(NUNIT):
            relu(0, u)
        for c in range(NPAIR):
            if c + 1 < NPAIR:
                relu(c + 1, 0)
            copy(c)
            if c + 1 < NPAIR:
                relu(c + 1, 1)
        for c in range(NPAIR):
            g.wait_ge(S["sC%d" % c], 2)
            g.remote_dma_fused([one(d, T.pl[:, t, hs(s), :], T.po[:, t, hs(s), :], S["pa%d" % t], m)
                                for d, t, m in _returns(topo, plan, i, kind, s, c)], local_sem=S.sent)

    if role < 2:
        for t in range(n):
            src = (i - t) % n
            got = 0
            for s in range(2):
                hit = [m for d, tt, m in _returns(topo, plan, src, role, s, t // 2) if tt == t and d == core]
                if hit:
                    got += _count(hit[0])
                else:
                    ve.wait_ge(S["sC%d" % (t // 2)], 2)
            ve.wait_ge(S["pa%d" % t], got)
            if t == 0:
                continue
            if t > 1:
                ve.wait_ge(S.sA, t - 1)
            out = T.yb[:] if t == n - 1 else T.ac[:, 0:NH, :]
            in0 = T.pl[:, 0] if t == 1 else T.ac[:, 0:NH, :]
            ve.tensor_tensor(out, in0, T.pl[:, t], AluOpType.add).then_inc(S.sA, 1)
        g.sync.wait_ge(S.sA, n - 1)
        g.sync.dma_start(T.y[:], T.yb[:]).then_inc(S.st, 16)
        g.sync.wait_ge(S.st, 16)

    g.wait_ge(S.sent, sent[0])
